import numpy as np
import ml_dtypes

BF16 = ml_dtypes.bfloat16


def bf(x):
    return np.asarray(x, np.float32).astype(BF16)


def f32(x):
    return np.asarray(x, np.float32)


def f64(x):
    return np.asarray(x).astype(np.float64)


def striped(idx):
    return np.tile(idx.reshape(-1, 16).T, (8, 1))


S, K, M, N = 512, 256, 512, 384


def gelu_tanh(v):
    return 0.5 * v * (1.0 + np.tanh(np.sqrt(2.0 / np.pi) * (v + 0.044715 * v**3)))


def setup_inputs():
    return {"base": bf(np.random.standard_normal((M, S))), "x": bf(np.random.standard_normal((K, N))), "w": bf(np.random.standard_normal((K, M)) / np.sqrt(K)), "b": f32(0.5 * np.random.standard_normal((M, 1))), "offs": striped(np.random.permutation(S)[:N])}


def reference(base, x, w, b, offs):
    idx = offs[:16].T.reshape(-1)
    z = f64(base).copy()
    z[:, idx] += f64(w).T @ f64(x)
    return gelu_tanh(z + f64(b))

@@ -1,0 +1,55 @@
+import concourse.mybir as mybir
+from concourse.masks import make_identity
+
+BF16, F32, U16 = mybir.dt.bfloat16, mybir.dt.float32, mybir.dt.uint16
+GELU_TANH = mybir.ActivationFunctionType.Gelu_apprx_tanh
+
+P = 128
+S, K, M, N = 512, 256, 512, 384
+FEATURE_BLOCKS = M // P
+K_BLOCKS = K // P
+
+FLOPS = 2 * K * M * N
+
+
+def tile_scatter_matmul_kernel(tc, base, x, w, b, offs, out):
+    nc = tc.nc
+    with (
+        tc.tile_pool(name="held", bufs=1) as held,
+        tc.psum_pool(name="windows", bufs=1) as windows,
+    ):
+        base_tile = held.tile([P, FEATURE_BLOCKS, S], BF16)
+        nc.sync.dma_start(base_tile[:], base.rearrange("(a p) s -> p a s", p=P))
+        offsets = held.tile([P, N // 16], U16)
+        nc.sync.dma_start(offsets[:], offs)
+        x_tile = held.tile([P, K_BLOCKS, N], BF16)
+        nc.sync.dma_start(x_tile[:], x.rearrange("(c p) n -> p c n", p=P))
+        w_tile = held.tile([P, K_BLOCKS, M], BF16)
+        nc.sync.dma_start(w_tile[:], w.rearrange("(c p) m -> p c m", p=P))
+
+        bias = held.tile([P, FEATURE_BLOCKS], F32)
+        nc.scalar.dma_start(bias[:], b.rearrange("(a p) o -> p (a o)", p=P))
+
+        identity = held.tile([P, P], BF16)
+        make_identity(nc, identity[:])
+
+        window = []
+        for a in range(FEATURE_BLOCKS):
+            block_window = windows.tile([P, S], F32, name=f"window{a}")
+            nc.tensor.matmul(block_window[:], identity[:], base_tile[:, a, :], start=True, stop=False)
+            window.append(block_window)
+
+        for a in range(FEATURE_BLOCKS):
+            for c in range(K_BLOCKS):
+                nc.tensor.matmul(
+                    window[a][:].indirect(offsets[:]),
+                    w_tile[:, c, a * P : (a + 1) * P],
+                    x_tile[:, c, :],
+                    start=False,
+                    stop=(c == K_BLOCKS - 1),
+                )
+
+        for a in range(FEATURE_BLOCKS):
+            result = held.tile([P, S], F32, name=f"result{a}")
+            nc.scalar.activation(result[:], window[a][:], GELU_TANH, bias=bias[:, a : a + 1])
+            nc.sync.dma_start(out[a * P : (a + 1) * P, :], result[:])

@@ -9,6 +9,8 @@ S, K, M, N = 512, 256, 512, 384
 FEATURE_BLOCKS = M // P
 K_BLOCKS = K // P
 
+WARM_UPS = 4
+
 FLOPS = 2 * K * M * N
 
 
@@ -18,8 +20,17 @@ def tile_scatter_matmul_kernel(tc, base, x, w, b, offs, out):
         tc.tile_pool(name="held", bufs=1) as held,
         tc.psum_pool(name="windows", bufs=1) as windows,
     ):
+        zeros = held.tile([P, P], BF16)
+        nc.vector.memset(zeros[:], 0.0)
+        spare = windows.tile([P, S], F32)
+        for warm_up in range(WARM_UPS):
+            nc.tensor.matmul(spare[:], zeros[:], zeros[:, 0:1].to_broadcast([P, S]), start=True, stop=True)
+        gelu_of_zero = held.tile([P, 1], F32)
+        nc.scalar.activation(gelu_of_zero[:], zeros[:, 0:1], GELU_TANH)
+
         base_tile = held.tile([P, FEATURE_BLOCKS, S], BF16)
-        nc.sync.dma_start(base_tile[:], base.rearrange("(a p) s -> p a s", p=P))
+        for a in range(FEATURE_BLOCKS):
+            nc.sync.dma_start(base_tile[:, a, :], base[a * P : (a + 1) * P, :])
         offsets = held.tile([P, N // 16], U16)
         nc.sync.dma_start(offsets[:], offs)
         x_tile = held.tile([P, K_BLOCKS, N], BF16)

@@ -20,6 +20,9 @@ def tile_scatter_matmul_kernel(tc, base, x, w, b, offs, out):
         tc.tile_pool(name="held", bufs=1) as held,
         tc.psum_pool(name="windows", bufs=1) as windows,
     ):
+        bias_rows = held.tile([FEATURE_BLOCKS, P], F32)
+        nc.scalar.dma_start(bias_rows[:], b.rearrange("(a p) o -> a (p o)", p=P))
+
         zeros = held.tile([P, P], BF16)
         nc.vector.memset(zeros[:], 0.0)
         spare = windows.tile([P, S], F32)
@@ -38,11 +41,15 @@ def tile_scatter_matmul_kernel(tc, base, x, w, b, offs, out):
         w_tile = held.tile([P, K_BLOCKS, M], BF16)
         nc.sync.dma_start(w_tile[:], w.rearrange("(c p) m -> p c m", p=P))
 
-        bias = held.tile([P, FEATURE_BLOCKS], F32)
-        nc.scalar.dma_start(bias[:], b.rearrange("(a p) o -> p (a o)", p=P))
-
         identity = held.tile([P, P], BF16)
         make_identity(nc, identity[:])
+        small_identity = held.tile([FEATURE_BLOCKS, FEATURE_BLOCKS], F32)
+        nc.vector.tensor_copy(small_identity[:], identity[0:FEATURE_BLOCKS, 0:FEATURE_BLOCKS])
+
+        bias_columns = windows.tile([P, FEATURE_BLOCKS], F32)
+        nc.tensor.matmul(bias_columns[:], bias_rows[:], small_identity[:], start=True, stop=True)
+        bias = held.tile([P, FEATURE_BLOCKS], F32)
+        nc.vector.tensor_copy(bias[:], bias_columns[:])
 
         window = []
         for a in range(FEATURE_BLOCKS):

@@ -39,7 +39,9 @@ def tile_scatter_matmul_kernel(tc, base, x, w, b, offs, out):
         x_tile = held.tile([P, K_BLOCKS, N], BF16)
         nc.sync.dma_start(x_tile[:], x.rearrange("(c p) n -> p c n", p=P))
         w_tile = held.tile([P, K_BLOCKS, M], BF16)
-        nc.sync.dma_start(w_tile[:], w.rearrange("(c p) m -> p c m", p=P))
+        w_blocks = w.rearrange("(c p) m -> p c m", p=P)
+        for half in (slice(0, M // 2), slice(M // 2, M)):
+            nc.sync.dma_start(w_tile[:, :, half], w_blocks[:, :, half])
 
         identity = held.tile([P, P], BF16)
         make_identity(nc, identity[:])
@@ -69,5 +71,9 @@ def tile_scatter_matmul_kernel(tc, base, x, w, b, offs, out):
 
         for a in range(FEATURE_BLOCKS):
             result = held.tile([P, S], F32, name=f"result{a}")
-            nc.scalar.activation(result[:], window[a][:], GELU_TANH, bias=bias[:, a : a + 1])
-            nc.sync.dma_start(out[a * P : (a + 1) * P, :], result[:])
+            pieces = 2 if a == FEATURE_BLOCKS - 1 else 1
+            width = S // pieces
+            for t in range(0, S, width):
+                columns = slice(t, t + width)
+                nc.scalar.activation(result[:, columns], window[a][:, columns], GELU_TANH, bias=bias[:, a : a + 1])
+                nc.sync.dma_start(out[a * P : (a + 1) * P, columns], result[:, columns])

import concourse.mybir as mybir
from concourse.masks import make_identity

BF16, F32, U16 = mybir.dt.bfloat16, mybir.dt.float32, mybir.dt.uint16
GELU_TANH = mybir.ActivationFunctionType.Gelu_apprx_tanh

P = 128
S, K, M, N = 512, 256, 512, 384
FEATURE_BLOCKS = M // P
K_BLOCKS = K // P

WARM_UPS = 4

FLOPS = 2 * K * M * N


def tile_scatter_matmul_kernel(tc, base, x, w, b, offs, out):
    nc = tc.nc
    with (
        tc.tile_pool(name="held", bufs=1) as held,
        tc.psum_pool(name="windows", bufs=1) as windows,
    ):
        bias_rows = held.tile([FEATURE_BLOCKS, P], F32)
        nc.scalar.dma_start(bias_rows[:], b.rearrange("(a p) o -> a (p o)", p=P))

        zeros = held.tile([P, P], BF16)
        nc.vector.memset(zeros[:], 0.0)
        spare = windows.tile([P, S], F32)
        for warm_up in range(WARM_UPS):
            nc.tensor.matmul(spare[:], zeros[:], zeros[:, 0:1].to_broadcast([P, S]), start=True, stop=True)
        gelu_of_zero = held.tile([P, 1], F32)
        nc.scalar.activation(gelu_of_zero[:], zeros[:, 0:1], GELU_TANH)

        base_tile = held.tile([P, FEATURE_BLOCKS, S], BF16)
        for a in range(FEATURE_BLOCKS):
            nc.sync.dma_start(base_tile[:, a, :], base[a * P : (a + 1) * P, :])
        offsets = held.tile([P, N // 16], U16)
        nc.sync.dma_start(offsets[:], offs)
        x_tile = held.tile([P, K_BLOCKS, N], BF16)
        nc.sync.dma_start(x_tile[:], x.rearrange("(c p) n -> p c n", p=P))
        w_tile = held.tile([P, K_BLOCKS, M], BF16)
        w_blocks = w.rearrange("(c p) m -> p c m", p=P)
        for half in (slice(0, M // 2), slice(M // 2, M)):
            nc.sync.dma_start(w_tile[:, :, half], w_blocks[:, :, half])

        identity = held.tile([P, P], BF16)
        make_identity(nc, identity[:])
        small_identity = held.tile([FEATURE_BLOCKS, FEATURE_BLOCKS], F32)
        nc.vector.tensor_copy(small_identity[:], identity[0:FEATURE_BLOCKS, 0:FEATURE_BLOCKS])

        bias_columns = windows.tile([P, FEATURE_BLOCKS], F32)
        nc.tensor.matmul(bias_columns[:], bias_rows[:], small_identity[:], start=True, stop=True)
        bias = held.tile([P, FEATURE_BLOCKS], F32)
        nc.vector.tensor_copy(bias[:], bias_columns[:])

        window = []
        for a in range(FEATURE_BLOCKS):
            block_window = windows.tile([P, S], F32, name=f"window{a}")
            nc.tensor.matmul(block_window[:], identity[:], base_tile[:, a, :], start=True, stop=False)
            window.append(block_window)

        for a in range(FEATURE_BLOCKS):
            for c in range(K_BLOCKS):
                nc.tensor.matmul(
                    window[a][:].indirect(offsets[:]),
                    w_tile[:, c, a * P : (a + 1) * P],
                    x_tile[:, c, :],
                    start=False,
                    stop=(c == K_BLOCKS - 1),
                )

        for a in range(FEATURE_BLOCKS):
            result = held.tile([P, S], F32, name=f"result{a}")
            pieces = 2 if a == FEATURE_BLOCKS - 1 else 1
            width = S // pieces
            for t in range(0, S, width):
                columns = slice(t, t + width)
                nc.scalar.activation(result[:, columns], window[a][:, columns], GELU_TANH, bias=bias[:, a : a + 1])
                nc.sync.dma_start(out[a * P : (a + 1) * P, columns], result[:, columns])
